import numpy as np
CORES = [10,11,138,139,266,267,394,395]
N = 8
def setup_inputs(rng):
    return {"x1": rng.standard_normal((N, 128, 8), dtype=np.float32), "x2": rng.standard_normal((N, 128, 128), dtype=np.float32)}
def reference(x1, x2):
    out = []
    g = np.concatenate(list(x1), axis=1)
    out.append(np.broadcast_to(g, (N,) + g.shape))
    s = x2.sum(axis=0, dtype=np.float64).astype(x2.dtype)
    b = 128 // N
    out.append(np.stack([s[:, r * b:(r + 1) * b] for r in range(N)]))
    return {"y1": out[0], "y2": out[1]}

@@ -1,0 +1,71 @@
+from concourse.bass import DstId, RemoteDMATransfer
+from concourse.mybir import AluOpType
+
+SCRATCH = {
+    "xs": ("sbuf", [128, 128], "float32"),
+    "ag": ("sbuf", [128, 64], "float32"),
+    "pl": ("sbuf", [128, 64], "float32"),
+    "rl": ("sbuf", [128, 32], "float32"),
+    "cl": ("sbuf", [128, 16], "float32"),
+}
+SEMAPHORES = ["ld1", "ld2", "y2c", "acc", "st1", "sent", "rs1", "rs2", "rs3", "ag1", "ag2", "ag3"]
+
+
+def rank_program(g, core, T, topo):
+    r = T.rank_of(core)
+    if r is None:
+        return
+    S = T.sem
+    h, p = r // 2, r % 2
+    R, C, D = h ^ 1, 3 - h, (h + 2) % 4
+
+    def dst(hh, pp):
+        rid, pid = topo.addr(T.cores[2 * hh + pp], core)
+        return DstId(rid=rid, pnc=pid)
+
+    def blk(t, k, w=16):
+        return t[:, w * k:w * (k + 1)]
+
+    def tr(to, mask, sem, srcs, out):
+        return RemoteDMATransfer(dst_ids=[to], dma_engine_mask=mask, remote_sem=sem, srcs=srcs, dsts=[out],
+                                 alu_op=1 if len(srcs) > 1 else 0)
+
+    g.scalar.dma_start(blk(T.ag, r, 8), T.x1[:]).then_inc(S.ld1, 16)
+    g.sync.dma_start(T.xs[:], T.x2[:]).then_inc(S.ld2, 16)
+    g.sync.dma_start(T.y2[:], blk(T.x2, r)).then_inc(S.y2c, 16)
+
+    g.wait_ge(S.ld1, 16)
+    g.remote_dma_fused([tr(dst(C, p), 0xFF, S.ag1, [blk(T.ag, r, 8)], blk(T.ag, r, 8))], local_sem=S.sent)
+    g.wait_ge(S.ld2, 16)
+    g.remote_dma_fused([tr(dst(h, 1 - p), 0xF << (4 * k), S.rs1, [blk(T.xs, 2 * k + 1 - p)], blk(T.pl, k))
+                        for k in range(4)], local_sem=S.sent)
+    g.wait_ge(S.rs1, 16)
+    g.remote_dma_fused([tr(dst(R, p), 0x0F, S.rs2, [blk(T.xs, 2 * R + p), blk(T.pl, R)], blk(T.rl, 0)),
+                        tr(dst(R, p), 0xF0, S.rs2, [blk(T.xs, 2 * D + p), blk(T.pl, D)], blk(T.rl, 1))],
+                       local_sem=S.sent)
+    g.wait_ge(S.y2c, 16)
+    g.dma_start(T.y2[:], blk(T.pl, h), accum_op=AluOpType.add).then_inc(S.acc, 16)
+    g.wait_ge(S.ag1, 8)
+    g.remote_dma_fused([tr(dst(R, p), 0x0F, S.ag2, [blk(T.ag, r, 8)], blk(T.ag, r, 8)),
+                        tr(dst(R, p), 0xF0, S.ag2, [blk(T.ag, 2 * C + p, 8)], blk(T.ag, 2 * C + p, 8))],
+                       local_sem=S.sent)
+    g.wait_ge(S.rs2, 8)
+    g.remote_dma_fused([tr(dst(C, p), 0xFF, S.rs3, [blk(T.xs, 2 * C + p), blk(T.pl, C), blk(T.rl, 1)], T.cl[:])],
+                       local_sem=S.sent)
+    g.wait_ge(S.acc, 16)
+    g.dma_start(T.y2[:], blk(T.rl, 0), accum_op=AluOpType.add).then_inc(S.acc, 16)
+    g.wait_ge(S.ag2, 8)
+    g.remote_dma_fused([tr(dst(h, 1 - p), 0xF << (4 * k), S.ag3, [blk(T.ag, 2 * k + p, 8)], blk(T.ag, 2 * k + p, 8))
+                        for k in range(4)], local_sem=S.sent)
+    g.scalar.wait_ge(S.ld1, 16)
+    g.scalar.wait_ge(S.ag1, 8)
+    g.scalar.wait_ge(S.ag2, 8)
+    g.scalar.wait_ge(S.ag3, 16)
+    g.scalar.dma_start(T.y1[:], T.ag[:]).then_inc(S.st1, 16)
+    g.wait_ge(S.acc, 32)
+    g.wait_ge(S.rs3, 8)
+    g.dma_start(T.y2[:], T.cl[:], accum_op=AluOpType.add).then_inc(S.acc, 16)
+    g.wait_ge(S.acc, 48)
+    g.wait_ge(S.ag3, 16)
+    g.wait_ge(S.sent, 64)
+    g.wait_ge(S.st1, 16)

@@ -2,70 +2,121 @@ from concourse.bass import DstId, RemoteDMATransfer
 from concourse.mybir import AluOpType
 
 SCRATCH = {
-    "xs": ("sbuf", [128, 128], "float32"),
-    "ag": ("sbuf", [128, 64], "float32"),
-    "pl": ("sbuf", [128, 64], "float32"),
-    "rl": ("sbuf", [128, 32], "float32"),
-    "cl": ("sbuf", [128, 16], "float32"),
+    "xb": ("dram", [7, 128, 16], "float32"),
+    "land": ("dram", [5, 128, 16], "float32"),
+    "ag": ("dram", [8, 128, 8], "float32"),
 }
-SEMAPHORES = ["ld1", "ld2", "y2c", "acc", "st1", "sent", "rs1", "rs2", "rs3", "ag1", "ag2", "ag3"]
+SEMAPHORES = ["ld1", "exa", "exb", "y2c", "acc", "st1", "sent", "h2", "h3", "f1", "f2", "f3", "a1", "a2", "a3"]
+
+H_R = (5, 7)
+H_D = (4, 0)
+H_C = (4, 6)
 
 
 def rank_program(g, core, T, topo):
-    r = T.rank_of(core)
-    if r is None:
-        return
     S = T.sem
-    h, p = r // 2, r % 2
+    h = topo.host(core)
+    base = [T.cores[2 * k] - T.cores[2 * k] % 8 for k in range(4)]
+    if core - core % 8 != base[h]:
+        return
+    c = core % 8
     R, C, D = h ^ 1, 3 - h, (h + 2) % 4
 
-    def dst(hh, pp):
-        rid, pid = topo.addr(T.cores[2 * hh + pp], core)
+    def to(world):
+        rid, pid = topo.addr(world, core)
         return DstId(rid=rid, pnc=pid)
 
-    def blk(t, k, w=16):
-        return t[:, w * k:w * (k + 1)]
-
-    def tr(to, mask, sem, srcs, out):
-        return RemoteDMATransfer(dst_ids=[to], dma_engine_mask=mask, remote_sem=sem, srcs=srcs, dsts=[out],
+    def tr(world, mask, sem, srcs, out):
+        return RemoteDMATransfer(dst_ids=[to(world)], dma_engine_mask=mask, remote_sem=sem, srcs=srcs, dsts=[out],
                                  alu_op=1 if len(srcs) > 1 else 0)
 
-    g.scalar.dma_start(blk(T.ag, r, 8), T.x1[:]).then_inc(S.ld1, 16)
-    g.sync.dma_start(T.xs[:], T.x2[:]).then_inc(S.ld2, 16)
-    g.sync.dma_start(T.y2[:], blk(T.x2, r)).then_inc(S.y2c, 16)
+    r = T.rank_of(core)
+    if r is None:
+        sent = 0
+        for p in range(2):
+            if c == H_R[p] or c == H_D[p]:
+                g.wait_ge(S.h2, 8)
+                if c == H_R[p]:
+                    t = tr(T.cores[2 * R + p], 0xFF, S.f2, [T.land[0], T.land[1]], T.land[1])
+                else:
+                    t = tr(base[R] + H_C[p], 0xFF, S.h3, [T.land[0], T.land[1]], T.land[4])
+                g.remote_dma_fused([t], local_sem=S.sent)
+                sent += 8
+        for p in range(2):
+            if c == H_C[p]:
+                g.wait_ge(S.h3, 16)
+                g.remote_dma_fused([tr(T.cores[2 * C + p], 0xFF, S.f3, [T.land[2], T.land[3], T.land[4]], T.land[2])],
+                                   local_sem=S.sent)
+                sent += 8
+        if sent:
+            g.wait_ge(S.sent, sent)
+        return
+
+    p = r % 2
+    q = 1 - p
+    mate = T.cores[2 * h + q]
+
+    def x2b(b):
+        return T.x2[:, 16 * b:16 * (b + 1)]
+
+    def y1p(j):
+        return T.y1[:, 8 * j:8 * (j + 1)]
+
+    g.scalar.dma_start(T.ag[r], T.x1[:]).then_inc(S.ld1, 16)
+    g.sync.dma_start(T.xb[0], x2b(2 * D)).then_inc(S.exa, 16)
+    g.scalar.dma_start(T.xb[1], x2b(2 * D + 1)).then_inc(S.exa, 16)
+    g.sync.dma_start(T.xb[2], x2b(2 * R)).then_inc(S.exa, 16)
+    g.scalar.dma_start(T.xb[3], x2b(2 * R + 1)).then_inc(S.exa, 16)
+    g.sync.dma_start(T.xb[4], x2b(2 * C)).then_inc(S.exb, 16)
+    g.scalar.dma_start(T.xb[5], x2b(2 * C + 1)).then_inc(S.exb, 16)
+    g.sync.dma_start(T.xb[6], x2b(2 * h + q)).then_inc(S.exb, 16)
+    g.scalar.dma_start(T.y2[:], x2b(r)).then_inc(S.y2c, 16)
+    g.sync.dma_start(y1p(r), T.x1[:]).then_inc(S.st1, 16)
 
     g.wait_ge(S.ld1, 16)
-    g.remote_dma_fused([tr(dst(C, p), 0xFF, S.ag1, [blk(T.ag, r, 8)], blk(T.ag, r, 8))], local_sem=S.sent)
-    g.wait_ge(S.ld2, 16)
-    g.remote_dma_fused([tr(dst(h, 1 - p), 0xF << (4 * k), S.rs1, [blk(T.xs, 2 * k + 1 - p)], blk(T.pl, k))
-                        for k in range(4)], local_sem=S.sent)
-    g.wait_ge(S.rs1, 16)
-    g.remote_dma_fused([tr(dst(R, p), 0x0F, S.rs2, [blk(T.xs, 2 * R + p), blk(T.pl, R)], blk(T.rl, 0)),
-                        tr(dst(R, p), 0xF0, S.rs2, [blk(T.xs, 2 * D + p), blk(T.pl, D)], blk(T.rl, 1))],
-                       local_sem=S.sent)
+    g.remote_dma_fused([tr(T.cores[2 * C + p], 0x000F, S.a1, [T.ag[r]], T.ag[r]),
+                        tr(T.cores[2 * R + p], 0x00F0, S.a1, [T.ag[r]], T.ag[r]),
+                        tr(mate, 0xFF00, S.a1, [T.ag[r]], T.ag[r])], local_sem=S.sent)
+    g.wait_ge(S.exa, 64)
+    g.remote_dma_fused([tr(base[h] + H_D[0], 0x000F, S.h2, [T.xb[0]], T.land[p]),
+                        tr(base[h] + H_D[1], 0x00F0, S.h2, [T.xb[1]], T.land[p]),
+                        tr(base[h] + H_R[0], 0x0F00, S.h2, [T.xb[2]], T.land[p]),
+                        tr(base[h] + H_R[1], 0xF000, S.h2, [T.xb[3]], T.land[p])], local_sem=S.sent)
+    g.wait_ge(S.exb, 48)
+    g.remote_dma_fused([tr(base[h] + H_C[0], 0x000F, S.h3, [T.xb[4]], T.land[2 + p]),
+                        tr(base[h] + H_C[1], 0x00F0, S.h3, [T.xb[5]], T.land[2 + p]),
+                        tr(mate, 0xFF00, S.f1, [T.xb[6]], T.land[0])], local_sem=S.sent)
+    jc, jr, jd = 2 * C + p, 2 * R + p, 2 * D + p
+    g.wait_ge(S.a1, 16)
+    g.remote_dma_fused([tr(T.cores[2 * R + p], 0x00FF, S.a2, [T.ag[jc]], T.ag[jc]),
+                        tr(mate, 0x0F00, S.a2, [T.ag[jc]], T.ag[jc]),
+                        tr(mate, 0xF000, S.a2, [T.ag[jr]], T.ag[jr])], local_sem=S.sent)
     g.wait_ge(S.y2c, 16)
-    g.dma_start(T.y2[:], blk(T.pl, h), accum_op=AluOpType.add).then_inc(S.acc, 16)
-    g.wait_ge(S.ag1, 8)
-    g.remote_dma_fused([tr(dst(R, p), 0x0F, S.ag2, [blk(T.ag, r, 8)], blk(T.ag, r, 8)),
-                        tr(dst(R, p), 0xF0, S.ag2, [blk(T.ag, 2 * C + p, 8)], blk(T.ag, 2 * C + p, 8))],
-                       local_sem=S.sent)
-    g.wait_ge(S.rs2, 8)
-    g.remote_dma_fused([tr(dst(C, p), 0xFF, S.rs3, [blk(T.xs, 2 * C + p), blk(T.pl, C), blk(T.rl, 1)], T.cl[:])],
-                       local_sem=S.sent)
+    g.wait_ge(S.f1, 8)
+    g.dma_start(T.y2[:], T.land[0], accum_op=AluOpType.add).then_inc(S.acc, 16)
+    g.wait_ge(S.a2, 16)
+    g.remote_dma_fused([tr(mate, 0xFFFF, S.a3, [T.ag[jd]], T.ag[jd])], local_sem=S.sent)
+
+    g.sync.wait_ge(S.a1, 16)
+    g.scalar.wait_ge(S.a1, 16)
+    g.sync.dma_start(y1p(2 * h + q), T.ag[2 * h + q]).then_inc(S.st1, 16)
+    g.scalar.dma_start(y1p(jr), T.ag[jr]).then_inc(S.st1, 16)
+    g.sync.dma_start(y1p(jc), T.ag[jc]).then_inc(S.st1, 16)
+    g.sync.wait_ge(S.a2, 16)
+    g.scalar.wait_ge(S.a2, 16)
+    g.sync.dma_start(y1p(jd), T.ag[jd]).then_inc(S.st1, 16)
+    g.scalar.dma_start(y1p(2 * C + q), T.ag[2 * C + q]).then_inc(S.st1, 16)
+    g.sync.dma_start(y1p(2 * R + q), T.ag[2 * R + q]).then_inc(S.st1, 16)
+    g.scalar.wait_ge(S.a3, 16)
+    g.scalar.dma_start(y1p(2 * D + q), T.ag[2 * D + q]).then_inc(S.st1, 16)
+
     g.wait_ge(S.acc, 16)
-    g.dma_start(T.y2[:], blk(T.rl, 0), accum_op=AluOpType.add).then_inc(S.acc, 16)
-    g.wait_ge(S.ag2, 8)
-    g.remote_dma_fused([tr(dst(h, 1 - p), 0xF << (4 * k), S.ag3, [blk(T.ag, 2 * k + p, 8)], blk(T.ag, 2 * k + p, 8))
-                        for k in range(4)], local_sem=S.sent)
-    g.scalar.wait_ge(S.ld1, 16)
-    g.scalar.wait_ge(S.ag1, 8)
-    g.scalar.wait_ge(S.ag2, 8)
-    g.scalar.wait_ge(S.ag3, 16)
-    g.scalar.dma_start(T.y1[:], T.ag[:]).then_inc(S.st1, 16)
+    g.wait_ge(S.f2, 8)
+    g.dma_start(T.y2[:], T.land[1], accum_op=AluOpType.add).then_inc(S.acc, 16)
     g.wait_ge(S.acc, 32)
-    g.wait_ge(S.rs3, 8)
-    g.dma_start(T.y2[:], T.cl[:], accum_op=AluOpType.add).then_inc(S.acc, 16)
+    g.wait_ge(S.f3, 8)
+    g.dma_start(T.y2[:], T.land[2], accum_op=AluOpType.add).then_inc(S.acc, 16)
     g.wait_ge(S.acc, 48)
-    g.wait_ge(S.ag3, 16)
-    g.wait_ge(S.sent, 64)
-    g.wait_ge(S.st1, 16)
+    g.wait_ge(S.a3, 16)
+    g.wait_ge(S.sent, 80)
+    g.wait_ge(S.st1, 128)

from concourse.bass import DstId, RemoteDMATransfer
from concourse.mybir import AluOpType

SCRATCH = {
    "xb": ("dram", [7, 128, 16], "float32"),
    "land": ("dram", [5, 128, 16], "float32"),
    "ag": ("dram", [8, 128, 8], "float32"),
}
SEMAPHORES = ["ld1", "exa", "exb", "y2c", "acc", "st1", "sent", "h2", "h3", "f1", "f2", "f3", "a1", "a2", "a3"]

H_R = (5, 7)
H_D = (4, 0)
H_C = (4, 6)


def rank_program(g, core, T, topo):
    S = T.sem
    h = topo.host(core)
    base = [T.cores[2 * k] - T.cores[2 * k] % 8 for k in range(4)]
    if core - core % 8 != base[h]:
        return
    c = core % 8
    R, C, D = h ^ 1, 3 - h, (h + 2) % 4

    def to(world):
        rid, pid = topo.addr(world, core)
        return DstId(rid=rid, pnc=pid)

    def tr(world, mask, sem, srcs, out):
        return RemoteDMATransfer(dst_ids=[to(world)], dma_engine_mask=mask, remote_sem=sem, srcs=srcs, dsts=[out],
                                 alu_op=1 if len(srcs) > 1 else 0)

    r = T.rank_of(core)
    if r is None:
        sent = 0
        for p in range(2):
            if c == H_R[p] or c == H_D[p]:
                g.wait_ge(S.h2, 8)
                if c == H_R[p]:
                    t = tr(T.cores[2 * R + p], 0xFF, S.f2, [T.land[0], T.land[1]], T.land[1])
                else:
                    t = tr(base[R] + H_C[p], 0xFF, S.h3, [T.land[0], T.land[1]], T.land[4])
                g.remote_dma_fused([t], local_sem=S.sent)
                sent += 8
        for p in range(2):
            if c == H_C[p]:
                g.wait_ge(S.h3, 16)
                g.remote_dma_fused([tr(T.cores[2 * C + p], 0xFF, S.f3, [T.land[2], T.land[3], T.land[4]], T.land[2])],
                                   local_sem=S.sent)
                sent += 8
        if sent:
            g.wait_ge(S.sent, sent)
        return

    p = r % 2
    q = 1 - p
    mate = T.cores[2 * h + q]

    def x2b(b):
        return T.x2[:, 16 * b:16 * (b + 1)]

    def y1p(j):
        return T.y1[:, 8 * j:8 * (j + 1)]

    g.scalar.dma_start(T.ag[r], T.x1[:]).then_inc(S.ld1, 16)
    g.sync.dma_start(T.xb[0], x2b(2 * D)).then_inc(S.exa, 16)
    g.scalar.dma_start(T.xb[1], x2b(2 * D + 1)).then_inc(S.exa, 16)
    g.sync.dma_start(T.xb[2], x2b(2 * R)).then_inc(S.exa, 16)
    g.scalar.dma_start(T.xb[3], x2b(2 * R + 1)).then_inc(S.exa, 16)
    g.sync.dma_start(T.xb[4], x2b(2 * C)).then_inc(S.exb, 16)
    g.scalar.dma_start(T.xb[5], x2b(2 * C + 1)).then_inc(S.exb, 16)
    g.sync.dma_start(T.xb[6], x2b(2 * h + q)).then_inc(S.exb, 16)
    g.scalar.dma_start(T.y2[:], x2b(r)).then_inc(S.y2c, 16)
    g.sync.dma_start(y1p(r), T.x1[:]).then_inc(S.st1, 16)

    g.wait_ge(S.ld1, 16)
    g.remote_dma_fused([tr(T.cores[2 * C + p], 0x000F, S.a1, [T.ag[r]], T.ag[r]),
                        tr(T.cores[2 * R + p], 0x00F0, S.a1, [T.ag[r]], T.ag[r]),
                        tr(mate, 0xFF00, S.a1, [T.ag[r]], T.ag[r])], local_sem=S.sent)
    g.wait_ge(S.exa, 64)
    g.remote_dma_fused([tr(base[h] + H_D[0], 0x000F, S.h2, [T.xb[0]], T.land[p]),
                        tr(base[h] + H_D[1], 0x00F0, S.h2, [T.xb[1]], T.land[p]),
                        tr(base[h] + H_R[0], 0x0F00, S.h2, [T.xb[2]], T.land[p]),
                        tr(base[h] + H_R[1], 0xF000, S.h2, [T.xb[3]], T.land[p])], local_sem=S.sent)
    g.wait_ge(S.exb, 48)
    g.remote_dma_fused([tr(base[h] + H_C[0], 0x000F, S.h3, [T.xb[4]], T.land[2 + p]),
                        tr(base[h] + H_C[1], 0x00F0, S.h3, [T.xb[5]], T.land[2 + p]),
                        tr(mate, 0xFF00, S.f1, [T.xb[6]], T.land[0])], local_sem=S.sent)
    jc, jr, jd = 2 * C + p, 2 * R + p, 2 * D + p
    g.wait_ge(S.a1, 16)
    g.remote_dma_fused([tr(T.cores[2 * R + p], 0x00FF, S.a2, [T.ag[jc]], T.ag[jc]),
                        tr(mate, 0x0F00, S.a2, [T.ag[jc]], T.ag[jc]),
                        tr(mate, 0xF000, S.a2, [T.ag[jr]], T.ag[jr])], local_sem=S.sent)
    g.wait_ge(S.y2c, 16)
    g.wait_ge(S.f1, 8)
    g.dma_start(T.y2[:], T.land[0], accum_op=AluOpType.add).then_inc(S.acc, 16)
    g.wait_ge(S.a2, 16)
    g.remote_dma_fused([tr(mate, 0xFFFF, S.a3, [T.ag[jd]], T.ag[jd])], local_sem=S.sent)

    g.sync.wait_ge(S.a1, 16)
    g.scalar.wait_ge(S.a1, 16)
    g.sync.dma_start(y1p(2 * h + q), T.ag[2 * h + q]).then_inc(S.st1, 16)
    g.scalar.dma_start(y1p(jr), T.ag[jr]).then_inc(S.st1, 16)
    g.sync.dma_start(y1p(jc), T.ag[jc]).then_inc(S.st1, 16)
    g.sync.wait_ge(S.a2, 16)
    g.scalar.wait_ge(S.a2, 16)
    g.sync.dma_start(y1p(jd), T.ag[jd]).then_inc(S.st1, 16)
    g.scalar.dma_start(y1p(2 * C + q), T.ag[2 * C + q]).then_inc(S.st1, 16)
    g.sync.dma_start(y1p(2 * R + q), T.ag[2 * R + q]).then_inc(S.st1, 16)
    g.scalar.wait_ge(S.a3, 16)
    g.scalar.dma_start(y1p(2 * D + q), T.ag[2 * D + q]).then_inc(S.st1, 16)

    g.wait_ge(S.acc, 16)
    g.wait_ge(S.f2, 8)
    g.dma_start(T.y2[:], T.land[1], accum_op=AluOpType.add).then_inc(S.acc, 16)
    g.wait_ge(S.acc, 32)
    g.wait_ge(S.f3, 8)
    g.dma_start(T.y2[:], T.land[2], accum_op=AluOpType.add).then_inc(S.acc, 16)
    g.wait_ge(S.acc, 48)
    g.wait_ge(S.a3, 16)
    g.wait_ge(S.sent, 80)
    g.wait_ge(S.st1, 128)
